import numpy as np
CORES = [11,27,43,59,75,91,107,123]
N = 8
def setup_inputs(rng):
    return {"x": rng.standard_normal((N, 128, 1024), dtype=np.float32)}
def reference(x):
    b = 1024 // N
    blocks = x.reshape(N, 128, N, b)
    return {"y": np.ascontiguousarray(blocks.transpose(2, 1, 0, 3)).reshape(N, 128, 1024)}

@@ -1,0 +1,75 @@
+from concourse.bass import DstId, RemoteDMATransfer
+
+B = 128
+
+SCRATCH = {
+    "xbuf": ("sbuf", [128, 1024], "float32"),
+    "land": ("sbuf", [128, 1024], "float32"),
+    "hbuf": ("sbuf", [128, 256], "float32"),
+}
+SEMAPHORES = ["ldA", "ldB", "go", "sent", "arrD", "arrH", "harr", "stored"]
+
+HELP_A = 4
+HELP_B = 5
+
+
+def blk(t, j, n=1):
+    return t[:, j * B:(j + n) * B]
+
+
+def xfer(topo, dst_core, dst_ap, src_ap, mask, sem):
+    rid, pid, se = topo.addr(dst_core)
+    return RemoteDMATransfer(dst_ids=[DstId(rid=rid, pnc=pid)], dma_engine_mask=mask, remote_sem=sem,
+                             src=src_ap, dst=dst_ap)
+
+
+def rank_program(g, core, T, topo):
+    S = T.sem
+    chip0 = topo.chip(core) * 8
+    k = core - chip0
+    r = T.rank_of(chip0 + 3)
+    if r is None:
+        return
+    p = r // 2
+    q = p ^ 1
+
+    if k == HELP_A:
+        g.wait_ge(S.harr, 8)
+        g.remote_dma_fused([xfer(topo, T.cores[2 * q + i], blk(T.land, r), blk(T.hbuf, i), 0xF << (4 * i), S.arrH)
+                            for i in range(2)], local_sem=S.sent)
+        g.wait_ge(S.sent, 8)
+        return
+    if k == HELP_B:
+        j = r ^ 1
+        rid, pid, se = topo.addr(T.cores[j])
+        g.wait_ge(S.harr, 8)
+        g.remote_dma(blk(T.land, r), blk(T.hbuf, j % 2), S.arrH, S.sent, pid, rid, 0xFF)
+        g.wait_ge(S.sent, 8)
+        return
+    if k != 3:
+        return
+
+    m0 = 4 * (r // 4)
+    o0 = 4 - m0
+    g.sync.dma_start(blk(T.xbuf, m0, 4), blk(T.x, m0, 4)).then_inc(S.ldA, 16)
+    g.scalar.dma_start(blk(T.xbuf, o0, 4), blk(T.x, o0, 4)).then_inc(S.ldB, 16)
+
+    g.wait_ge(S.ldA, 16)
+    g.remote_dma_fused([xfer(topo, chip0 + HELP_A, T.hbuf[:, :], blk(T.xbuf, 2 * q, 2), 0x00FF, S.harr),
+                        xfer(topo, chip0 + HELP_B, T.hbuf[:, :], blk(T.xbuf, 2 * p, 2), 0xFF00, S.harr)],
+                       local_sem=S.sent)
+    g.wait_ge(S.ldB, 16)
+    g.remote_dma_fused([xfer(topo, T.cores[o0 + i], blk(T.land, r), blk(T.xbuf, o0 + i), 0x3 << (2 * i), S.arrD)
+                        for i in range(4)], local_sem=S.sent)
+    g.sem_inc(S.go, 1)
+
+    g.sync.wait_ge(S.arrD, 8)
+    g.sync.dma_start(blk(T.y, o0, 4), blk(T.land, o0, 4)).then_inc(S.stored, 16)
+
+    g.scalar.wait_ge(S.go, 1)
+    g.scalar.dma_start(blk(T.land, r), blk(T.x, r)).then_inc(S.arrH, 16)
+    g.scalar.wait_ge(S.arrH, 32)
+    g.scalar.dma_start(blk(T.y, m0, 4), blk(T.land, m0, 4)).then_inc(S.stored, 16)
+
+    g.wait_ge(S.sent, 24)
+    g.wait_ge(S.stored, 32)

@@ -7,7 +7,7 @@ SCRATCH = {
     "land": ("sbuf", [128, 1024], "float32"),
     "hbuf": ("sbuf", [128, 256], "float32"),
 }
-SEMAPHORES = ["ldA", "ldB", "go", "sent", "arrD", "arrH", "harr", "stored"]
+SEMAPHORES = ["ldH", "ld1", "ld2", "go", "sent", "arr1", "arr2", "arrA", "arrB", "harr", "stored"]
 
 HELP_A = 4
 HELP_B = 5
@@ -15,6 +15,10 @@ HELP_B = 5
 
 def blk(t, j, n=1):
     return t[:, j * B:(j + n) * B]
+
+
+def pair(t, i):
+    return t[:, 2 * i * B:(2 * i + 2) * B]
 
 
 def xfer(topo, dst_core, dst_ap, src_ap, mask, sem):
@@ -35,7 +39,7 @@ def rank_program(g, core, T, topo):
 
     if k == HELP_A:
         g.wait_ge(S.harr, 8)
-        g.remote_dma_fused([xfer(topo, T.cores[2 * q + i], blk(T.land, r), blk(T.hbuf, i), 0xF << (4 * i), S.arrH)
+        g.remote_dma_fused([xfer(topo, T.cores[2 * q + i], blk(T.land, r), blk(T.hbuf, i), 0xF << (4 * i), S.arrA)
                             for i in range(2)], local_sem=S.sent)
         g.wait_ge(S.sent, 8)
         return
@@ -43,33 +47,41 @@ def rank_program(g, core, T, topo):
         j = r ^ 1
         rid, pid, se = topo.addr(T.cores[j])
         g.wait_ge(S.harr, 8)
-        g.remote_dma(blk(T.land, r), blk(T.hbuf, j % 2), S.arrH, S.sent, pid, rid, 0xFF)
+        g.remote_dma(blk(T.land, r), blk(T.hbuf, j % 2), S.arrB, S.sent, pid, rid, 0xFF)
         g.wait_ge(S.sent, 8)
         return
     if k != 3:
         return
 
-    m0 = 4 * (r // 4)
-    o0 = 4 - m0
-    g.sync.dma_start(blk(T.xbuf, m0, 4), blk(T.x, m0, 4)).then_inc(S.ldA, 16)
-    g.scalar.dma_start(blk(T.xbuf, o0, 4), blk(T.x, o0, 4)).then_inc(S.ldB, 16)
+    o1 = 2 * (1 - r // 4) + p % 2
+    o2 = o1 ^ 1
 
-    g.wait_ge(S.ldA, 16)
-    g.remote_dma_fused([xfer(topo, chip0 + HELP_A, T.hbuf[:, :], blk(T.xbuf, 2 * q, 2), 0x00FF, S.harr),
-                        xfer(topo, chip0 + HELP_B, T.hbuf[:, :], blk(T.xbuf, 2 * p, 2), 0xFF00, S.harr)],
+    g.sync.dma_start(pair(T.xbuf, q), pair(T.x, q)).then_inc(S.ldH, 16)
+    g.scalar.dma_start(pair(T.xbuf, p), pair(T.x, p)).then_inc(S.ldH, 16)
+    g.sync.dma_start(pair(T.xbuf, o1), pair(T.x, o1)).then_inc(S.ld1, 16)
+    g.scalar.dma_start(pair(T.xbuf, o2), pair(T.x, o2)).then_inc(S.ld2, 16)
+
+    g.wait_ge(S.ldH, 32)
+    g.remote_dma_fused([xfer(topo, chip0 + HELP_A, T.hbuf[:, :], pair(T.xbuf, q), 0x00FF, S.harr),
+                        xfer(topo, chip0 + HELP_B, T.hbuf[:, :], pair(T.xbuf, p), 0xFF00, S.harr)],
                        local_sem=S.sent)
-    g.wait_ge(S.ldB, 16)
-    g.remote_dma_fused([xfer(topo, T.cores[o0 + i], blk(T.land, r), blk(T.xbuf, o0 + i), 0x3 << (2 * i), S.arrD)
-                        for i in range(4)], local_sem=S.sent)
+    for o, ld, arr in ((o1, S.ld1, S.arr1), (o2, S.ld2, S.arr2)):
+        g.wait_ge(ld, 16)
+        g.remote_dma_fused([xfer(topo, T.cores[2 * o + i], blk(T.land, r), blk(T.xbuf, 2 * o + i), 0xF << (4 * i), arr)
+                            for i in range(2)], local_sem=S.sent)
     g.sem_inc(S.go, 1)
 
-    g.sync.wait_ge(S.arrD, 8)
-    g.sync.dma_start(blk(T.y, o0, 4), blk(T.land, o0, 4)).then_inc(S.stored, 16)
+    g.sync.wait_ge(S.arr1, 8)
+    g.sync.dma_start(pair(T.y, o1), pair(T.land, o1)).then_inc(S.stored, 16)
+    g.sync.wait_ge(S.arr2, 8)
+    g.sync.dma_start(pair(T.y, o2), pair(T.land, o2)).then_inc(S.stored, 16)
 
     g.scalar.wait_ge(S.go, 1)
-    g.scalar.dma_start(blk(T.land, r), blk(T.x, r)).then_inc(S.arrH, 16)
-    g.scalar.wait_ge(S.arrH, 32)
-    g.scalar.dma_start(blk(T.y, m0, 4), blk(T.land, m0, 4)).then_inc(S.stored, 16)
+    g.scalar.dma_start(blk(T.land, r), blk(T.x, r)).then_inc(S.arrB, 16)
+    g.scalar.wait_ge(S.arrB, 24)
+    g.scalar.dma_start(pair(T.y, p), pair(T.land, p)).then_inc(S.stored, 16)
+    g.scalar.wait_ge(S.arrA, 8)
+    g.scalar.dma_start(pair(T.y, q), pair(T.land, q)).then_inc(S.stored, 16)
 
-    g.wait_ge(S.sent, 24)
-    g.wait_ge(S.stored, 32)
+    g.wait_ge(S.sent, 32)
+    g.wait_ge(S.stored, 64)

@@ -6,11 +6,11 @@ SCRATCH = {
     "xbuf": ("sbuf", [128, 1024], "float32"),
     "land": ("sbuf", [128, 1024], "float32"),
     "hbuf": ("sbuf", [128, 256], "float32"),
+    "rbuf": ("sbuf", [128, 128], "float32"),
 }
-SEMAPHORES = ["ldH", "ld1", "ld2", "go", "sent", "arr1", "arr2", "arrA", "arrB", "harr", "stored"]
+SEMAPHORES = ["ldQ", "ldN", "ld1", "ld2", "go", "sent", "arr1", "arr2", "arrA", "arrB", "harr", "stored"]
 
 HELP_A = 4
-HELP_B = 5
 
 
 def blk(t, j, n=1):
@@ -27,27 +27,36 @@ def xfer(topo, dst_core, dst_ap, src_ap, mask, sem):
                              src=src_ap, dst=dst_ap)
 
 
+def send(g, topo, dst_core, dst_ap, src_ap, mask, remote_sem, local_sem):
+    rid, pid, se = topo.addr(dst_core)
+    g.remote_dma(dst_ap, src_ap, remote_sem, local_sem, pid, rid, mask)
+
+
 def rank_program(g, core, T, topo):
     S = T.sem
     chip0 = topo.chip(core) * 8
     k = core - chip0
+
+    if k == 3 and T.rank_of(core) is None:
+        j = T.rank_of(core + 8)
+        if j is None:
+            return
+        g.wait_ge(S.harr, 8)
+        send(g, topo, core + 8, blk(T.land, j ^ 1), T.rbuf[:, :], 0xFF, S.arrB, S.sent)
+        g.wait_ge(S.sent, 8)
+        return
+
     r = T.rank_of(chip0 + 3)
     if r is None:
         return
     p = r // 2
     q = p ^ 1
+    n = r ^ 1
 
     if k == HELP_A:
-        g.wait_ge(S.harr, 8)
+        g.wait_ge(S.harr, 16)
         g.remote_dma_fused([xfer(topo, T.cores[2 * q + i], blk(T.land, r), blk(T.hbuf, i), 0xF << (4 * i), S.arrA)
                             for i in range(2)], local_sem=S.sent)
-        g.wait_ge(S.sent, 8)
-        return
-    if k == HELP_B:
-        j = r ^ 1
-        rid, pid, se = topo.addr(T.cores[j])
-        g.wait_ge(S.harr, 8)
-        g.remote_dma(blk(T.land, r), blk(T.hbuf, j % 2), S.arrB, S.sent, pid, rid, 0xFF)
         g.wait_ge(S.sent, 8)
         return
     if k != 3:
@@ -56,15 +65,15 @@ def rank_program(g, core, T, topo):
     o1 = 2 * (1 - r // 4) + p % 2
     o2 = o1 ^ 1
 
-    g.sync.dma_start(pair(T.xbuf, q), pair(T.x, q)).then_inc(S.ldH, 16)
-    g.scalar.dma_start(pair(T.xbuf, p), pair(T.x, p)).then_inc(S.ldH, 16)
+    g.sync.dma_start(pair(T.xbuf, q), pair(T.x, q)).then_inc(S.ldQ, 16)
+    g.scalar.dma_start(blk(T.xbuf, n), blk(T.x, n)).then_inc(S.ldN, 16)
     g.sync.dma_start(pair(T.xbuf, o1), pair(T.x, o1)).then_inc(S.ld1, 16)
     g.scalar.dma_start(pair(T.xbuf, o2), pair(T.x, o2)).then_inc(S.ld2, 16)
 
-    g.wait_ge(S.ldH, 32)
-    g.remote_dma_fused([xfer(topo, chip0 + HELP_A, T.hbuf[:, :], pair(T.xbuf, q), 0x00FF, S.harr),
-                        xfer(topo, chip0 + HELP_B, T.hbuf[:, :], pair(T.xbuf, p), 0xFF00, S.harr)],
-                       local_sem=S.sent)
+    g.wait_ge(S.ldQ, 16)
+    send(g, topo, chip0 + HELP_A, T.hbuf[:, :], pair(T.xbuf, q), 0xFFFF, S.harr, S.sent)
+    g.wait_ge(S.ldN, 16)
+    send(g, topo, T.cores[n] - 8, T.rbuf[:, :], blk(T.xbuf, n), 0xFF, S.harr, S.sent)
     for o, ld, arr in ((o1, S.ld1, S.arr1), (o2, S.ld2, S.arr2)):
         g.wait_ge(ld, 16)
         g.remote_dma_fused([xfer(topo, T.cores[2 * o + i], blk(T.land, r), blk(T.xbuf, 2 * o + i), 0xF << (4 * i), arr)
@@ -83,5 +92,5 @@ def rank_program(g, core, T, topo):
     g.scalar.wait_ge(S.arrA, 8)
     g.scalar.dma_start(pair(T.y, q), pair(T.land, q)).then_inc(S.stored, 16)
 
-    g.wait_ge(S.sent, 32)
+    g.wait_ge(S.sent, 40)
     g.wait_ge(S.stored, 64)

@@ -5,12 +5,11 @@ B = 128
 SCRATCH = {
     "xbuf": ("sbuf", [128, 1024], "float32"),
     "land": ("sbuf", [128, 1024], "float32"),
-    "hbuf": ("sbuf", [128, 256], "float32"),
-    "rbuf": ("sbuf", [128, 128], "float32"),
+    "hbuf": ("sbuf", [128, 128], "float32"),
 }
 SEMAPHORES = ["ldQ", "ldN", "ld1", "ld2", "go", "sent", "arr1", "arr2", "arrA", "arrB", "harr", "stored"]
 
-HELP_A = 4
+HELP = 4
 
 
 def blk(t, j, n=1):
@@ -32,6 +31,12 @@ def send(g, topo, dst_core, dst_ap, src_ap, mask, remote_sem, local_sem):
     g.remote_dma(dst_ap, src_ap, remote_sem, local_sem, pid, rid, mask)
 
 
+def pass_on(g, topo, T, dst_core, src_rank, arr):
+    g.wait_ge(T.sem.harr, 8)
+    send(g, topo, dst_core, blk(T.land, src_rank), T.hbuf[:, :], 0xFF, arr, T.sem.sent)
+    g.wait_ge(T.sem.sent, 8)
+
+
 def rank_program(g, core, T, topo):
     S = T.sem
     chip0 = topo.chip(core) * 8
@@ -39,11 +44,8 @@ def rank_program(g, core, T, topo):
 
     if k == 3 and T.rank_of(core) is None:
         j = T.rank_of(core + 8)
-        if j is None:
-            return
-        g.wait_ge(S.harr, 8)
-        send(g, topo, core + 8, blk(T.land, j ^ 1), T.rbuf[:, :], 0xFF, S.arrB, S.sent)
-        g.wait_ge(S.sent, 8)
+        if j is not None:
+            pass_on(g, topo, T, core + 8, j ^ 1, S.arrB)
         return
 
     r = T.rank_of(chip0 + 3)
@@ -53,11 +55,8 @@ def rank_program(g, core, T, topo):
     q = p ^ 1
     n = r ^ 1
 
-    if k == HELP_A:
-        g.wait_ge(S.harr, 16)
-        g.remote_dma_fused([xfer(topo, T.cores[2 * q + i], blk(T.land, r), blk(T.hbuf, i), 0xF << (4 * i), S.arrA)
-                            for i in range(2)], local_sem=S.sent)
-        g.wait_ge(S.sent, 8)
+    if k == HELP or k == HELP + 1:
+        pass_on(g, topo, T, T.cores[2 * q + k - HELP], r, S.arrA)
         return
     if k != 3:
         return
@@ -71,9 +70,10 @@ def rank_program(g, core, T, topo):
     g.scalar.dma_start(pair(T.xbuf, o2), pair(T.x, o2)).then_inc(S.ld2, 16)
 
     g.wait_ge(S.ldQ, 16)
-    send(g, topo, chip0 + HELP_A, T.hbuf[:, :], pair(T.xbuf, q), 0xFFFF, S.harr, S.sent)
+    g.remote_dma_fused([xfer(topo, chip0 + HELP + i, T.hbuf[:, :], blk(T.xbuf, 2 * q + i), 0xFF << (8 * i), S.harr)
+                        for i in range(2)], local_sem=S.sent)
     g.wait_ge(S.ldN, 16)
-    send(g, topo, T.cores[n] - 8, T.rbuf[:, :], blk(T.xbuf, n), 0xFF, S.harr, S.sent)
+    send(g, topo, T.cores[n] - 8, T.hbuf[:, :], blk(T.xbuf, n), 0xFF, S.harr, S.sent)
     for o, ld, arr in ((o1, S.ld1, S.arr1), (o2, S.ld2, S.arr2)):
         g.wait_ge(ld, 16)
         g.remote_dma_fused([xfer(topo, T.cores[2 * o + i], blk(T.land, r), blk(T.xbuf, 2 * o + i), 0xF << (4 * i), arr)
@@ -86,11 +86,11 @@ def rank_program(g, core, T, topo):
     g.sync.dma_start(pair(T.y, o2), pair(T.land, o2)).then_inc(S.stored, 16)
 
     g.scalar.wait_ge(S.go, 1)
-    g.scalar.dma_start(blk(T.land, r), blk(T.x, r)).then_inc(S.arrB, 16)
-    g.scalar.wait_ge(S.arrB, 24)
-    g.scalar.dma_start(pair(T.y, p), pair(T.land, p)).then_inc(S.stored, 16)
-    g.scalar.wait_ge(S.arrA, 8)
+    g.scalar.dma_start(blk(T.y, r), blk(T.x, r)).then_inc(S.stored, 16)
+    g.scalar.wait_ge(S.arrB, 8)
+    g.scalar.dma_start(blk(T.y, n), blk(T.land, n)).then_inc(S.stored, 16)
+    g.scalar.wait_ge(S.arrA, 16)
     g.scalar.dma_start(pair(T.y, q), pair(T.land, q)).then_inc(S.stored, 16)
 
     g.wait_ge(S.sent, 40)
-    g.wait_ge(S.stored, 64)
+    g.wait_ge(S.stored, 80)

@@ -87,10 +87,10 @@ def rank_program(g, core, T, topo):
 
     g.scalar.wait_ge(S.go, 1)
     g.scalar.dma_start(blk(T.y, r), blk(T.x, r)).then_inc(S.stored, 16)
-    g.scalar.wait_ge(S.arrB, 8)
-    g.scalar.dma_start(blk(T.y, n), blk(T.land, n)).then_inc(S.stored, 16)
     g.scalar.wait_ge(S.arrA, 16)
     g.scalar.dma_start(pair(T.y, q), pair(T.land, q)).then_inc(S.stored, 16)
+    g.scalar.wait_ge(S.arrB, 8)
+    g.scalar.dma_start(blk(T.y, n), blk(T.land, n)).then_inc(S.stored, 16)
 
     g.wait_ge(S.sent, 40)
     g.wait_ge(S.stored, 80)

from concourse.bass import DstId, RemoteDMATransfer

B = 128

SCRATCH = {
    "xbuf": ("sbuf", [128, 1024], "float32"),
    "land": ("sbuf", [128, 1024], "float32"),
    "hbuf": ("sbuf", [128, 128], "float32"),
}
SEMAPHORES = ["ldQ", "ldN", "ld1", "ld2", "go", "sent", "arr1", "arr2", "arrA", "arrB", "harr", "stored"]

HELP = 4


def blk(t, j, n=1):
    return t[:, j * B:(j + n) * B]


def pair(t, i):
    return t[:, 2 * i * B:(2 * i + 2) * B]


def xfer(topo, dst_core, dst_ap, src_ap, mask, sem):
    rid, pid, se = topo.addr(dst_core)
    return RemoteDMATransfer(dst_ids=[DstId(rid=rid, pnc=pid)], dma_engine_mask=mask, remote_sem=sem,
                             src=src_ap, dst=dst_ap)


def send(g, topo, dst_core, dst_ap, src_ap, mask, remote_sem, local_sem):
    rid, pid, se = topo.addr(dst_core)
    g.remote_dma(dst_ap, src_ap, remote_sem, local_sem, pid, rid, mask)


def pass_on(g, topo, T, dst_core, src_rank, arr):
    g.wait_ge(T.sem.harr, 8)
    send(g, topo, dst_core, blk(T.land, src_rank), T.hbuf[:, :], 0xFF, arr, T.sem.sent)
    g.wait_ge(T.sem.sent, 8)


def rank_program(g, core, T, topo):
    S = T.sem
    chip0 = topo.chip(core) * 8
    k = core - chip0

    if k == 3 and T.rank_of(core) is None:
        j = T.rank_of(core + 8)
        if j is not None:
            pass_on(g, topo, T, core + 8, j ^ 1, S.arrB)
        return

    r = T.rank_of(chip0 + 3)
    if r is None:
        return
    p = r // 2
    q = p ^ 1
    n = r ^ 1

    if k == HELP or k == HELP + 1:
        pass_on(g, topo, T, T.cores[2 * q + k - HELP], r, S.arrA)
        return
    if k != 3:
        return

    o1 = 2 * (1 - r // 4) + p % 2
    o2 = o1 ^ 1

    g.sync.dma_start(pair(T.xbuf, q), pair(T.x, q)).then_inc(S.ldQ, 16)
    g.scalar.dma_start(blk(T.xbuf, n), blk(T.x, n)).then_inc(S.ldN, 16)
    g.sync.dma_start(pair(T.xbuf, o1), pair(T.x, o1)).then_inc(S.ld1, 16)
    g.scalar.dma_start(pair(T.xbuf, o2), pair(T.x, o2)).then_inc(S.ld2, 16)

    g.wait_ge(S.ldQ, 16)
    g.remote_dma_fused([xfer(topo, chip0 + HELP + i, T.hbuf[:, :], blk(T.xbuf, 2 * q + i), 0xFF << (8 * i), S.harr)
                        for i in range(2)], local_sem=S.sent)
    g.wait_ge(S.ldN, 16)
    send(g, topo, T.cores[n] - 8, T.hbuf[:, :], blk(T.xbuf, n), 0xFF, S.harr, S.sent)
    for o, ld, arr in ((o1, S.ld1, S.arr1), (o2, S.ld2, S.arr2)):
        g.wait_ge(ld, 16)
        g.remote_dma_fused([xfer(topo, T.cores[2 * o + i], blk(T.land, r), blk(T.xbuf, 2 * o + i), 0xF << (4 * i), arr)
                            for i in range(2)], local_sem=S.sent)
    g.sem_inc(S.go, 1)

    g.sync.wait_ge(S.arr1, 8)
    g.sync.dma_start(pair(T.y, o1), pair(T.land, o1)).then_inc(S.stored, 16)
    g.sync.wait_ge(S.arr2, 8)
    g.sync.dma_start(pair(T.y, o2), pair(T.land, o2)).then_inc(S.stored, 16)

    g.scalar.wait_ge(S.go, 1)
    g.scalar.dma_start(blk(T.y, r), blk(T.x, r)).then_inc(S.stored, 16)
    g.scalar.wait_ge(S.arrA, 16)
    g.scalar.dma_start(pair(T.y, q), pair(T.land, q)).then_inc(S.stored, 16)
    g.scalar.wait_ge(S.arrB, 8)
    g.scalar.dma_start(blk(T.y, n), blk(T.land, n)).then_inc(S.stored, 16)

    g.wait_ge(S.sent, 40)
    g.wait_ge(S.stored, 80)
